import numpy as np
import ml_dtypes


def mxq(x, axis, fmt="e4m3"):
    dtype, down = {"e4m3": (ml_dtypes.float8_e4m3fn, 7), "e5m2": (ml_dtypes.float8_e5m2, 14)}[fmt]
    v = np.moveaxis(np.asarray(x, np.float32).astype(ml_dtypes.bfloat16).astype(np.float64), axis, -1)
    blocks = v.reshape(v.shape[:-1] + (-1, 32))
    amax = np.abs(blocks).max(-1, keepdims=True)
    byte = np.maximum(np.where(amax > 0, np.frexp(amax)[1] - 1 + 127, 0) - down, 1)
    scale = np.exp2(byte - 127.0)
    codes = (blocks / scale).astype(np.float32).astype(dtype).astype(np.float64)
    return np.moveaxis((codes * scale).reshape(v.shape), -1, axis)


WIDE = False


def mx_kscale(k):
    if not WIDE:
        return np.ones(k)
    levels = np.array([10, -10, 5, -5, 0])
    if k % 512:
        return np.exp2(np.random.permutation(np.resize(levels, k // 32))).repeat(32)
    a = np.empty((k // 512, 16))
    for p in range(k // 512):
        a[p, :8] = np.random.permutation(np.resize(levels, 8))
        for g in range(8):
            far = levels[np.abs(levels - a[p, g]) >= 10]
            a[p, g + 8] = far[np.random.randint(len(far))]
    return np.exp2(a.ravel()).repeat(32)


def f64(x):
    return np.asarray(x).astype(np.float64)


def striped(idx):
    return np.tile(idx.reshape(-1, 16).T, (8, 1)).astype(np.uint16)


def unstriped(offs):
    return offs[:16].T.reshape(-1).astype(np.int64)


def striped8(idx):
    return np.concatenate([x.reshape(-1, 16).T for x in idx]).astype(np.uint16)


def runs(offs, k):
    lists = np.stack([offs[16 * r : 16 * r + 16].T.reshape(-1) for r in range(8)]).astype(np.int64)
    return lists[np.arange(k) % 512 // 64]


def pack_weight(w):
    k, n = w.shape
    w = f64(np.asarray(w, np.float32).astype(ml_dtypes.bfloat16)).reshape(k // 32, 32, n)
    amax = np.abs(w).max(1)
    byte = np.clip(np.where(amax > 0, np.frexp(amax)[1] - 1 + 127 - 7, 1), 1, 254)
    scaled = (w * np.exp2(127.0 - byte)[:, None, :]).reshape(k, n).astype(np.float32)
    words = np.ascontiguousarray(scaled.reshape(k // 512, 128, 4, n).transpose(0, 1, 3, 2)).astype(ml_dtypes.float8_e4m3fn).view(np.uint8)
    return words, np.ascontiguousarray(byte.astype(np.uint8).reshape(k // 512, 16, n))


def unpack_weight(words, scales):
    g, p, n, _ = words.shape
    vals = np.ascontiguousarray(words).view(ml_dtypes.float8_e4m3fn).astype(np.float64) * np.repeat(np.exp2(scales.astype(np.float64) - 127.0), 8, axis=1)[..., None]
    return vals.transpose(0, 1, 3, 2).reshape(g * 512, n)


E2M1 = np.array([0.0, 0.5, 1.0, 1.5, 2.0, 3.0, 4.0, 6.0, -0.0, -0.5, -1.0, -1.5, -2.0, -3.0, -4.0, -6.0])


def pack_fp4(w):
    k, n = w.shape
    w = f64(np.asarray(w, np.float32).astype(ml_dtypes.bfloat16)).reshape(k // 32, 32, n)
    amax = np.abs(w).max(1)
    mant, ex = np.frexp(amax / 6.0)
    byte = np.clip(np.where(amax > 0, np.where(mant > 0.5, ex, ex - 1) + 127, 1), 1, 254)
    scaled = (w * np.exp2(127.0 - byte)[:, None, :]).reshape(k, n).astype(np.float32)
    c = np.ascontiguousarray(scaled.reshape(k // 512, 128, 4, n).transpose(0, 1, 3, 2)).astype(ml_dtypes.float4_e2m1fn).view(np.uint8) & 0xF
    words = (c[..., 0::2] | (c[..., 1::2] << 4)).reshape(k // 512, 128, 2 * n)
    return np.ascontiguousarray(words), np.ascontiguousarray(byte.astype(np.uint8).reshape(k // 512, 16, n))


def unpack_fp4(words, scales):
    g, _, n = scales.shape
    words = np.ascontiguousarray(words).reshape(g, 128, n, 2)
    nib = np.empty((g, 128, n, 4), np.uint8)
    nib[..., 0::2] = words & 0xF
    nib[..., 1::2] = words >> 4
    vals = E2M1[nib] * np.repeat(np.exp2(scales.astype(np.float64) - 127.0), 8, axis=1)[..., None]
    return vals.transpose(0, 1, 3, 2).reshape(g * 512, n)


def planes(y):
    n, m = y.shape
    v = y.astype(np.float32).astype(ml_dtypes.bfloat16).astype(np.float64).reshape(n // 32, 32, m)
    top = np.abs(v).max(1)
    byte = np.clip(np.where(top > 0, np.frexp(top)[1] - 1 + 127 - 7, 1), 1, 254)
    codes = (v * np.exp2(127.0 - byte)[:, None, :]).reshape(n, m).astype(np.float32).astype(ml_dtypes.float8_e4m3fn).view(np.uint8)
    words = codes.reshape(n // 512, 128, 4, m).transpose(0, 1, 3, 2)
    return np.ascontiguousarray(words), np.ascontiguousarray(byte.astype(np.uint8).reshape(n // 512, 16, m))


K, T, S, V, H, C = 512, 2048, 512, 256, 512, 512


def setup_inputs():
    n = np.random.standard_normal
    s = mx_kscale(K)[:, None]
    packed_xT = pack_weight(n((K, T)) * s)
    packed_w1 = pack_fp4(n((K, H)) / np.sqrt(K) / s)
    packed_w2 = pack_fp4(n((K, H)) / np.sqrt(K) / s)
    return {
        "x_words": packed_xT[0],
        "x_scales": packed_xT[1],
        "w1_words": packed_w1[0],
        "w1_scales": packed_w1[1],
        "w2_words": packed_w2[0],
        "w2_scales": packed_w2[1],
        "gs": (np.random.uniform(0.5, 1.5, (K, 1)) / s).astype(np.float32),
        "offs": striped(np.random.permutation(T)[:S]),
        "two": striped(np.random.permutation(T)[:S]),
        "sub_l": striped8(np.stack([np.random.permutation(S)[:V] for _ in range(8)])),
        "enz": striped8(np.stack([np.random.permutation(S)[:V] for _ in range(8)])),
        "inh": striped8(np.stack([np.random.permutation(S)[:V] for _ in range(8)])),
        "cand": striped(np.random.permutation(T)[:C]),
    }


def reference(x_words, x_scales, w1_words, w1_scales, w2_words, w2_scales, gs, offs, two, sub_l, enz, inh, cand):
    x_cand = unpack_weight(x_words, x_scales)[:, unstriped(cand)]
    xq = unpack_weight(x_words, x_scales)[:, unstriped(offs)]
    y = unpack_fp4(w1_words, w1_scales).T @ xq
    x_two = unpack_weight(x_words, x_scales)[:, unstriped(two)]
    c = ((unpack_fp4(w2_words, w2_scales).T @ x_two)) ** 2
    sb = c[np.arange(H)[:, None], runs(sub_l, H)]
    z = f64(gs) * (((y[np.arange(H)[:, None], runs(enz, H)]) * sb) / (sb + 0.5 + c[np.arange(H)[:, None], runs(inh, H)]))
    out_0 = 0.0625 * ((x_cand.T @ mxq(z, 0, "e4m3")))
    return (out_0,) + planes(out_0)

@@ -1,0 +1,181 @@
+from contextlib import ExitStack
+
+import concourse.mybir as mybir
+
+K, T, S, V, H, C = 512, 2048, 512, 256, 512, 512
+FLOPS = 2 * K * H * S * 2 + 2 * K * C * V
+
+F32 = mybir.dt.float32
+BF16 = mybir.dt.bfloat16
+I32 = mybir.dt.int32
+U32 = mybir.dt.uint32
+U16 = mybir.dt.uint16
+U8 = mybir.dt.uint8
+FP8X4 = mybir.dt.float8_e4m3fn_x4
+FP4X4 = mybir.dt.float4_e2m1fn_x4
+ACT = mybir.ActivationFunctionType
+ALU = mybir.AluOpType
+
+P = 128
+PACK = 4
+HALF = V // 2
+
+
+def tile_picked_enzyme_none_po_kernel(tc, x_words, x_scales, w1_words, w1_scales, w2_words, w2_scales, gs, offs, two, sub_l, enz, inh, cand, out_0, out_1, out_2):
+    nc = tc.nc
+    with ExitStack() as ctx:
+        keep = ctx.enter_context(tc.tile_pool(name="keep", bufs=1))
+        psum = ctx.enter_context(tc.psum_pool(name="psum", bufs=8))
+
+        def load_scale_rows(plane, rows, queue):
+            for q in range(4):
+                queue.dma_start(plane[32 * q : 32 * q + 4, :].bitcast(I32), rows[0, 4 * q : 4 * q + 4, :].bitcast(I32))
+
+        def load_list(src, name):
+            t = keep.tile(list(src.shape), U16, name=name)
+            nc.sync.dma_start(t[:], src)
+            return t
+
+        xs = keep.tile([P, T], U8, name="xs", align_bytes=64)
+        nc.gpsimd.memset(xs[:].bitcast(I32), 0)
+        w2s_raw = keep.tile([P, H], U8, name="w2s_raw", align_bytes=64)
+        w1s_raw = keep.tile([P, H], U8, name="w1s_raw", align_bytes=64)
+        nc.vector.memset(w2s_raw[:].bitcast(I32), 0)
+        nc.vector.memset(w1s_raw[:].bitcast(I32), 0)
+
+        w2w_raw = keep.tile([P, 2 * H], U8, name="w2w_raw", align_bytes=64)
+        nc.sync.dma_start(w2w_raw[:].bitcast(I32), w2_words[0].bitcast(I32))
+        w1w_raw = keep.tile([P, 2 * H], U8, name="w1w_raw", align_bytes=64)
+        nc.sync.dma_start(w1w_raw[:].bitcast(I32), w1_words[0].bitcast(I32))
+        load_scale_rows(xs, x_scales, nc.sync)
+        two_l = load_list(two, "two_l")
+        offs_l = load_list(offs, "offs_l")
+        load_scale_rows(w2s_raw, w2_scales, nc.sync)
+        cand_l = load_list(cand, "cand_l")
+        xw = keep.tile([P, T], I32, name="xw", align_bytes=64)
+        nc.sync.dma_start(xw[:], x_words[0].rearrange("p n t -> p (n t)").bitcast(I32))
+        load_scale_rows(w1s_raw, w1_scales, nc.sync)
+        sub_t = load_list(sub_l, "sub_t")
+        inh_t = load_list(inh, "inh_t")
+        enz_t = load_list(enz, "enz_t")
+        gs_t = keep.tile([P, PACK], F32, name="gs_t")
+        nc.sync.dma_start(gs_t[:], gs.rearrange("(p t) o -> p (t o)", t=PACK))
+
+        def gather_bytes(lst, name):
+            t = keep.tile([P, S], U8, name=name, align_bytes=64)
+            nc.vector.tensor_copy(t[:], xs[:].indirect(lst[:]))
+            return t
+
+        def gather_words(lst, name):
+            t = keep.tile([P, S], U32, name=name, align_bytes=64)
+            nc.vector.tensor_copy(t[:], xw[:].bitcast(U32).indirect(lst[:]))
+            return t
+
+        def deal_fp4(raw, name):
+            t = keep.tile([P, 2 * H], U8, name=name, align_bytes=64)
+            nc.vector.tensor_copy(t[:].rearrange("p (t m b) -> p t m b", t=PACK, b=2), raw[:].rearrange("p (m t b) -> p t m b", t=PACK, b=2))
+            return t
+
+        def deal_bytes(raw, name):
+            t = keep.tile([P, S], U8, name=name, align_bytes=64)
+            nc.vector.tensor_copy(t[:].rearrange("p (t m) -> p t m", t=PACK), raw[:].rearrange("p (m t) -> p t m", t=PACK))
+            return t
+
+        w2w = deal_fp4(w2w_raw, "w2w")
+        w1w = deal_fp4(w1w_raw, "w1w")
+        two_s = gather_bytes(two_l, "two_s")
+        offs_s = gather_bytes(offs_l, "offs_s")
+        w2s = deal_bytes(w2s_raw, "w2s")
+        cand_s_raw = gather_bytes(cand_l, "cand_s_raw")
+        two_w = gather_words(two_l, "two_w")
+        w1s = deal_bytes(w1s_raw, "w1s")
+        offs_w = gather_words(offs_l, "offs_w")
+
+        def project(ww, ws, xg_w, xg_s, t):
+            acc = psum.tile([P, S], F32, name="acc")
+            nc.tensor.matmul_mx(
+                out=acc[:],
+                lhsT=ww[:, 2 * P * t : 2 * P * (t + 1)].bitcast(FP4X4),
+                lhsT_scale=ws[:, P * t : P * (t + 1)],
+                rhs=xg_w[:].bitcast(FP8X4),
+                rhs_scale=xg_s[:],
+                start=True,
+                stop=True,
+            )
+            return acc
+
+        c_tiles, y_tiles = [], []
+        for t in range(PACK):
+            acc = project(w2w, w2s, two_w, two_s, t)
+            c_t = keep.tile([P, S], F32, name="c%d" % t)
+            nc.scalar.activation(c_t[:], acc[:], ACT.Square)
+            c_tiles.append(c_t)
+        for t in range(PACK):
+            acc = project(w1w, w1s, offs_w, offs_s, t)
+            y_t = keep.tile([P, S], F32, name="y%d" % t)
+            nc.scalar.activation(y_t[:], acc[:], ACT.Copy, scale=gs_t[:, t : t + 1])
+            y_tiles.append(y_t)
+
+        cand_w = keep.tile([P, C], U32, name="cand_w", align_bytes=64)
+        nc.vector.tensor_copy(cand_w[:].rearrange("p (t m) -> p m t", t=PACK), xw[:].bitcast(U32).indirect(cand_l[:]))
+        cand_s = deal_bytes(cand_s_raw, "cand_s")
+
+        sb = keep.tile([P, PACK, V], F32, name="sb")
+        tot = keep.tile([P, PACK, V], F32, name="tot", tag="w1w", align_bytes=64)
+        root = keep.tile([P, PACK, V], F32, name="root")
+        inv = keep.tile([P, PACK, V], F32, name="inv")
+        for t in range(PACK):
+            nc.vector.tensor_copy(sb[:, t, :], c_tiles[t][:].indirect(sub_t[:]))
+        for t in range(PACK):
+            nc.vector.tensor_tensor(tot[:, t, :], c_tiles[t][:].indirect(inh_t[:]), sb[:, t, :], ALU.add)
+            nc.scalar.activation(root[:, t, :], tot[:, t, :], ACT.Abs_reciprocal_sqrt, bias=0.5)
+            nc.scalar.activation(inv[:, t, :], root[:, t, :], ACT.Square)
+
+        z_codes = keep.tile([P, V], U32, name="z_codes", align_bytes=64)
+        z_scales = keep.tile([P, V], U8, name="z_scales", align_bytes=64)
+        o_codes = keep.tile([P, V], U32, name="o_codes", align_bytes=64)
+        o_scales = keep.tile([P, V], U8, name="o_scales", align_bytes=64)
+        out_rows = out_0.rearrange("(p t) v -> p t v", t=PACK)
+        words_out = out_1[0].rearrange("p n t -> p (n t)").bitcast(I32)
+        accs = []
+        for h in range(2):
+            cols = slice(h * HALF, (h + 1) * HALF)
+            num = keep.tile([P, PACK, HALF], F32, name="num%d" % h, tag=("num", "root")[h])
+            for t in range(PACK):
+                nc.vector.tensor_tensor(num[:, t, :], y_tiles[t][:].indirect(enz_t[:, h * (HALF // 16) : (h + 1) * (HALF // 16)]), sb[:, t, cols], ALU.mult)
+            z_h = keep.tile([P, HALF * PACK], BF16, name="z16_%d" % h, align_bytes=64)
+            nc.vector.tensor_tensor(
+                z_h[:].rearrange("p (c i t) -> p c t i", i=4, t=PACK),
+                num[:].rearrange("p t (c i) -> p c t i", i=4),
+                inv[:, :, cols].rearrange("p t (c i) -> p c t i", i=4),
+                ALU.mult,
+            )
+            nc.vector.quantize_mx(out=z_codes[:, cols].bitcast(FP8X4), scales=z_scales[:, cols], in_=z_h[:])
+            acc = psum.tile([P, S], F32, name="acc")
+            for t in range(PACK):
+                nc.tensor.matmul_mx(
+                    out=acc[:, t * HALF : (t + 1) * HALF],
+                    lhsT=cand_w[:, P * t : P * (t + 1)].bitcast(FP8X4),
+                    lhsT_scale=cand_s[:, P * t : P * (t + 1)],
+                    rhs=z_codes[:, cols].bitcast(FP8X4),
+                    rhs_scale=z_scales[:, cols],
+                    start=True,
+                    stop=True,
+                )
+            accs.append(acc)
+        for h in range(2):
+            cols = slice(h * HALF, (h + 1) * HALF)
+            o16 = keep.tile([P, HALF * PACK], BF16, name="o16_%d" % h, align_bytes=64)
+            nc.scalar.activation(
+                o16[:].rearrange("p (v t) -> p v t", t=PACK),
+                accs[h][:].rearrange("p (t v) -> p v t", t=PACK),
+                ACT.Copy,
+                scale=0.0625,
+            )
+            o32 = keep.tile([P, PACK, HALF], F32, name="o32_%d" % h)
+            nc.scalar.activation(o32[:].rearrange("p t v -> p (t v)"), accs[h][:], ACT.Copy, scale=0.0625)
+            nc.scalar.dma_start(out_rows[:, :, cols], o32[:])
+            nc.vector.quantize_mx(out=o_codes[:, cols].bitcast(FP8X4), scales=o_scales[:, cols], in_=o16[:])
+            nc.sync.dma_start(words_out[:, cols], o_codes[:, cols].bitcast(I32))
+        for q in range(4):
+            nc.sync.dma_start(out_2[0, 4 * q : 4 * q + 4, :].bitcast(I32), o_scales[32 * q : 32 * q + 4, :].bitcast(I32))

@@ -37,37 +37,42 @@ def tile_picked_enzyme_none_po_kernel(tc, x_words, x_scales, w1_words, w1_scales
             return t
 
         xs = keep.tile([P, T], U8, name="xs", align_bytes=64)
-        nc.gpsimd.memset(xs[:].bitcast(I32), 0)
+        nc.vector.memset(xs[:, : T // 2].bitcast(I32), 0)
+        nc.gpsimd.memset(xs[:, T // 2 :].bitcast(I32), 0)
         w2s_raw = keep.tile([P, H], U8, name="w2s_raw", align_bytes=64)
         w1s_raw = keep.tile([P, H], U8, name="w1s_raw", align_bytes=64)
         nc.vector.memset(w2s_raw[:].bitcast(I32), 0)
         nc.vector.memset(w1s_raw[:].bitcast(I32), 0)
+        one = keep.tile([P, 1], F32, name="one")
+        nc.vector.memset(one[:], 1.0)
+        warm = keep.tile([P, 1], F32, name="warm")
+        nc.scalar.activation(warm[:], one[:], ACT.Abs_reciprocal_sqrt, bias=0.5)
 
         w2w_raw = keep.tile([P, 2 * H], U8, name="w2w_raw", align_bytes=64)
         nc.sync.dma_start(w2w_raw[:].bitcast(I32), w2_words[0].bitcast(I32))
-        w1w_raw = keep.tile([P, 2 * H], U8, name="w1w_raw", align_bytes=64)
-        nc.sync.dma_start(w1w_raw[:].bitcast(I32), w1_words[0].bitcast(I32))
         load_scale_rows(xs, x_scales, nc.sync)
         two_l = load_list(two, "two_l")
         offs_l = load_list(offs, "offs_l")
-        load_scale_rows(w2s_raw, w2_scales, nc.sync)
+        w1w_raw = keep.tile([P, 2 * H], U8, name="w1w_raw", align_bytes=64)
+        nc.sync.dma_start(w1w_raw[:].bitcast(I32), w1_words[0].bitcast(I32))
         cand_l = load_list(cand, "cand_l")
         xw = keep.tile([P, T], I32, name="xw", align_bytes=64)
         nc.sync.dma_start(xw[:], x_words[0].rearrange("p n t -> p (n t)").bitcast(I32))
+        load_scale_rows(w2s_raw, w2_scales, nc.sync)
         load_scale_rows(w1s_raw, w1_scales, nc.sync)
         sub_t = load_list(sub_l, "sub_t")
         inh_t = load_list(inh, "inh_t")
-        enz_t = load_list(enz, "enz_t")
         gs_t = keep.tile([P, PACK], F32, name="gs_t")
         nc.sync.dma_start(gs_t[:], gs.rearrange("(p t) o -> p (t o)", t=PACK))
+        enz_t = load_list(enz, "enz_t")
 
         def gather_bytes(lst, name):
             t = keep.tile([P, S], U8, name=name, align_bytes=64)
             nc.vector.tensor_copy(t[:], xs[:].indirect(lst[:]))
             return t
 
-        def gather_words(lst, name):
-            t = keep.tile([P, S], U32, name=name, align_bytes=64)
+        def gather_words(lst, name, tag):
+            t = keep.tile([P, S], U32, name=name, tag=tag, align_bytes=64)
             nc.vector.tensor_copy(t[:], xw[:].bitcast(U32).indirect(lst[:]))
             return t
 
@@ -76,8 +81,8 @@ def tile_picked_enzyme_none_po_kernel(tc, x_words, x_scales, w1_words, w1_scales
             nc.vector.tensor_copy(t[:].rearrange("p (t m b) -> p t m b", t=PACK, b=2), raw[:].rearrange("p (m t b) -> p t m b", t=PACK, b=2))
             return t
 
-        def deal_bytes(raw, name):
-            t = keep.tile([P, S], U8, name=name, align_bytes=64)
+        def deal_bytes(raw, name, tag):
+            t = keep.tile([P, S], U8, name=name, tag=tag, align_bytes=64)
             nc.vector.tensor_copy(t[:].rearrange("p (t m) -> p t m", t=PACK), raw[:].rearrange("p (m t) -> p t m", t=PACK))
             return t
 
@@ -85,11 +90,11 @@ def tile_picked_enzyme_none_po_kernel(tc, x_words, x_scales, w1_words, w1_scales
         w1w = deal_fp4(w1w_raw, "w1w")
         two_s = gather_bytes(two_l, "two_s")
         offs_s = gather_bytes(offs_l, "offs_s")
-        w2s = deal_bytes(w2s_raw, "w2s")
+        w2s = deal_bytes(w2s_raw, "w2s", "w2s")
         cand_s_raw = gather_bytes(cand_l, "cand_s_raw")
-        two_w = gather_words(two_l, "two_w")
-        w1s = deal_bytes(w1s_raw, "w1s")
-        offs_w = gather_words(offs_l, "offs_w")
+        two_w = gather_words(two_l, "two_w", "two_w")
+        w1s = deal_bytes(w1s_raw, "w1s", "w1s")
+        offs_w = gather_words(offs_l, "offs_w", "w2s_raw")
 
         def project(ww, ws, xg_w, xg_s, t):
             acc = psum.tile([P, S], F32, name="acc")
@@ -116,9 +121,7 @@ def tile_picked_enzyme_none_po_kernel(tc, x_words, x_scales, w1_words, w1_scales
             nc.scalar.activation(y_t[:], acc[:], ACT.Copy, scale=gs_t[:, t : t + 1])
             y_tiles.append(y_t)
 
-        cand_w = keep.tile([P, C], U32, name="cand_w", align_bytes=64)
-        nc.vector.tensor_copy(cand_w[:].rearrange("p (t m) -> p m t", t=PACK), xw[:].bitcast(U32).indirect(cand_l[:]))
-        cand_s = deal_bytes(cand_s_raw, "cand_s")
+        cand_s = deal_bytes(cand_s_raw, "cand_s", "w1s_raw")
 
         sb = keep.tile([P, PACK, V], F32, name="sb")
         tot = keep.tile([P, PACK, V], F32, name="tot", tag="w1w", align_bytes=64)
@@ -130,6 +133,13 @@ def tile_picked_enzyme_none_po_kernel(tc, x_words, x_scales, w1_words, w1_scales
             nc.vector.tensor_tensor(tot[:, t, :], c_tiles[t][:].indirect(inh_t[:]), sb[:, t, :], ALU.add)
             nc.scalar.activation(root[:, t, :], tot[:, t, :], ACT.Abs_reciprocal_sqrt, bias=0.5)
             nc.scalar.activation(inv[:, t, :], root[:, t, :], ACT.Square)
+        cand_w_raw = keep.tile([P, C], U32, name="cand_w_raw", tag="w2s_raw", align_bytes=64)
+        nc.vector.tensor_copy(cand_w_raw[:], xw[:].bitcast(U32).indirect(cand_l[:]))
+        cand_w = keep.tile([P, C], I32, name="cand_w", align_bytes=64)
+        nc.vector.tensor_copy(
+            cand_w[:].rearrange("p (t c i) -> p c t i", t=PACK, i=4),
+            cand_w_raw[:].bitcast(I32).rearrange("p (c i t) -> p c t i", t=PACK, i=4),
+        )
 
         z_codes = keep.tile([P, V], U32, name="z_codes", align_bytes=64)
         z_scales = keep.tile([P, V], U8, name="z_scales", align_bytes=64)
@@ -145,16 +155,17 @@ def tile_picked_enzyme_none_po_kernel(tc, x_words, x_scales, w1_words, w1_scales
                 nc.vector.tensor_tensor(num[:, t, :], y_tiles[t][:].indirect(enz_t[:, h * (HALF // 16) : (h + 1) * (HALF // 16)]), sb[:, t, cols], ALU.mult)
             z_h = keep.tile([P, HALF * PACK], BF16, name="z16_%d" % h, align_bytes=64)
             nc.vector.tensor_tensor(
-                z_h[:].rearrange("p (c i t) -> p c t i", i=4, t=PACK),
-                num[:].rearrange("p t (c i) -> p c t i", i=4),
-                inv[:, :, cols].rearrange("p t (c i) -> p c t i", i=4),
+                z_h[:].rearrange("p (c i t) -> p c t i", i=2, t=PACK),
+                num[:].rearrange("p t (c i) -> p c t i", i=2),
+                inv[:, :, cols].rearrange("p t (c i) -> p c t i", i=2),
                 ALU.mult,
             )
             nc.vector.quantize_mx(out=z_codes[:, cols].bitcast(FP8X4), scales=z_scales[:, cols], in_=z_h[:])
-            acc = psum.tile([P, S], F32, name="acc")
+            banks = [psum.tile([P, S], F32, name="acc") for b in range(h + 1)]
+            per_bank = PACK // len(banks)
             for t in range(PACK):
                 nc.tensor.matmul_mx(
-                    out=acc[:, t * HALF : (t + 1) * HALF],
+                    out=banks[t // per_bank][:, (t % per_bank) * HALF : (t % per_bank + 1) * HALF],
                     lhsT=cand_w[:, P * t : P * (t + 1)].bitcast(FP8X4),
                     lhsT_scale=cand_s[:, P * t : P * (t + 1)],
                     rhs=z_codes[:, cols].bitcast(FP8X4),
@@ -162,20 +173,23 @@ def tile_picked_enzyme_none_po_kernel(tc, x_words, x_scales, w1_words, w1_scales
                     start=True,
                     stop=True,
                 )
-            accs.append(acc)
+            accs.append(banks)
         for h in range(2):
             cols = slice(h * HALF, (h + 1) * HALF)
+            banks = accs[h]
+            per_bank = PACK // len(banks)
+            o32 = keep.tile([P, PACK * HALF], F32, name="o32_%d" % h)
+            for b, bank in enumerate(banks):
+                nc.scalar.activation(o32[:, b * per_bank * HALF : (b + 1) * per_bank * HALF], bank[:, : per_bank * HALF], ACT.Copy, scale=0.0625)
+            nc.scalar.dma_start(out_rows[:, :, cols], o32[:].rearrange("p (t v) -> p t v", t=PACK))
             o16 = keep.tile([P, HALF * PACK], BF16, name="o16_%d" % h, align_bytes=64)
-            nc.scalar.activation(
-                o16[:].rearrange("p (v t) -> p v t", t=PACK),
-                accs[h][:].rearrange("p (t v) -> p v t", t=PACK),
-                ACT.Copy,
-                scale=0.0625,
-            )
-            o32 = keep.tile([P, PACK, HALF], F32, name="o32_%d" % h)
-            nc.scalar.activation(o32[:].rearrange("p t v -> p (t v)"), accs[h][:], ACT.Copy, scale=0.0625)
-            nc.scalar.dma_start(out_rows[:, :, cols], o32[:])
+            o16_v = o16[:].rearrange("p (c i t) -> p c t i", i=2, t=PACK)
+            o32_v = o32[:].rearrange("p (t c i) -> p c t i", i=2, t=PACK)
+            if h == 0:
+                nc.scalar.copy(o16_v, o32_v)
+            else:
+                nc.vector.tensor_copy(o16_v, o32_v)
             nc.vector.quantize_mx(out=o_codes[:, cols].bitcast(FP8X4), scales=o_scales[:, cols], in_=o16[:])
             nc.sync.dma_start(words_out[:, cols], o_codes[:, cols].bitcast(I32))
         for q in range(4):
-            nc.sync.dma_start(out_2[0, 4 * q : 4 * q + 4, :].bitcast(I32), o_scales[32 * q : 32 * q + 4, :].bitcast(I32))
+            (nc.sync, nc.scalar)[q % 2].dma_start(out_2[0, 4 * q : 4 * q + 4, :].bitcast(I32), o_scales[32 * q : 32 * q + 4, :].bitcast(I32))

@@ -37,8 +37,7 @@ def tile_picked_enzyme_none_po_kernel(tc, x_words, x_scales, w1_words, w1_scales
             return t
 
         xs = keep.tile([P, T], U8, name="xs", align_bytes=64)
-        nc.vector.memset(xs[:, : T // 2].bitcast(I32), 0)
-        nc.gpsimd.memset(xs[:, T // 2 :].bitcast(I32), 0)
+        nc.vector.memset(xs[:].bitcast(I32), 0)
         w2s_raw = keep.tile([P, H], U8, name="w2s_raw", align_bytes=64)
         w1s_raw = keep.tile([P, H], U8, name="w1s_raw", align_bytes=64)
         nc.vector.memset(w2s_raw[:].bitcast(I32), 0)
@@ -50,15 +49,15 @@ def tile_picked_enzyme_none_po_kernel(tc, x_words, x_scales, w1_words, w1_scales
 
         w2w_raw = keep.tile([P, 2 * H], U8, name="w2w_raw", align_bytes=64)
         nc.sync.dma_start(w2w_raw[:].bitcast(I32), w2_words[0].bitcast(I32))
-        load_scale_rows(xs, x_scales, nc.sync)
-        two_l = load_list(two, "two_l")
-        offs_l = load_list(offs, "offs_l")
         w1w_raw = keep.tile([P, 2 * H], U8, name="w1w_raw", align_bytes=64)
         nc.sync.dma_start(w1w_raw[:].bitcast(I32), w1_words[0].bitcast(I32))
+        two_l = load_list(two, "two_l")
+        load_scale_rows(xs, x_scales, nc.sync)
+        offs_l = load_list(offs, "offs_l")
         cand_l = load_list(cand, "cand_l")
+        load_scale_rows(w2s_raw, w2_scales, nc.sync)
         xw = keep.tile([P, T], I32, name="xw", align_bytes=64)
         nc.sync.dma_start(xw[:], x_words[0].rearrange("p n t -> p (n t)").bitcast(I32))
-        load_scale_rows(w2s_raw, w2_scales, nc.sync)
         load_scale_rows(w1s_raw, w1_scales, nc.sync)
         sub_t = load_list(sub_l, "sub_t")
         inh_t = load_list(inh, "inh_t")
@@ -95,6 +94,7 @@ def tile_picked_enzyme_none_po_kernel(tc, x_words, x_scales, w1_words, w1_scales
         two_w = gather_words(two_l, "two_w", "two_w")
         w1s = deal_bytes(w1s_raw, "w1s", "w1s")
         offs_w = gather_words(offs_l, "offs_w", "w2s_raw")
+        cand_w_raw = gather_words(cand_l, "cand_w_raw", "w1s_raw")
 
         def project(ww, ws, xg_w, xg_s, t):
             acc = psum.tile([P, S], F32, name="acc")
@@ -115,31 +115,65 @@ def tile_picked_enzyme_none_po_kernel(tc, x_words, x_scales, w1_words, w1_scales
             c_t = keep.tile([P, S], F32, name="c%d" % t)
             nc.scalar.activation(c_t[:], acc[:], ACT.Square)
             c_tiles.append(c_t)
-        for t in range(PACK):
-            acc = project(w1w, w1s, offs_w, offs_s, t)
+        y_accs = [project(w1w, w1s, offs_w, offs_s, t) for t in range(PACK)]
+
+        def scale_y(t):
             y_t = keep.tile([P, S], F32, name="y%d" % t)
-            nc.scalar.activation(y_t[:], acc[:], ACT.Copy, scale=gs_t[:, t : t + 1])
+            nc.scalar.activation(y_t[:], y_accs[t][:], ACT.Copy, scale=gs_t[:, t : t + 1])
             y_tiles.append(y_t)
 
-        cand_s = deal_bytes(cand_s_raw, "cand_s", "w1s_raw")
+        for t in range(PACK - 1):
+            scale_y(t)
 
         sb = keep.tile([P, PACK, V], F32, name="sb")
         tot = keep.tile([P, PACK, V], F32, name="tot", tag="w1w", align_bytes=64)
-        root = keep.tile([P, PACK, V], F32, name="root")
-        inv = keep.tile([P, PACK, V], F32, name="inv")
+        roots = [keep.tile([P, 2, V], F32, name="root%d" % u, align_bytes=64) for u in range(2)]
+        invs = [keep.tile([P, 2, V], F32, name="inv%d" % u) for u in range(2)]
         for t in range(PACK):
             nc.vector.tensor_copy(sb[:, t, :], c_tiles[t][:].indirect(sub_t[:]))
         for t in range(PACK):
             nc.vector.tensor_tensor(tot[:, t, :], c_tiles[t][:].indirect(inh_t[:]), sb[:, t, :], ALU.add)
-            nc.scalar.activation(root[:, t, :], tot[:, t, :], ACT.Abs_reciprocal_sqrt, bias=0.5)
-            nc.scalar.activation(inv[:, t, :], root[:, t, :], ACT.Square)
-        cand_w_raw = keep.tile([P, C], U32, name="cand_w_raw", tag="w2s_raw", align_bytes=64)
-        nc.vector.tensor_copy(cand_w_raw[:], xw[:].bitcast(U32).indirect(cand_l[:]))
-        cand_w = keep.tile([P, C], I32, name="cand_w", align_bytes=64)
+            nc.scalar.activation(roots[t // 2][:, t % 2, :], tot[:, t, :], ACT.Abs_reciprocal_sqrt, bias=0.5)
+            nc.scalar.activation(invs[t // 2][:, t % 2, :], roots[t // 2][:, t % 2, :], ACT.Square)
+        scale_y(PACK - 1)
+
+        rate = keep.tile([P, PACK, V], F32, name="rate")
+        z32 = [keep.tile([P, PACK, HALF], F32, name="z32_0"), None]
+
+        def speeds_times_rates(h, t):
+            nc.vector.tensor_tensor(
+                z32[h][:, t, :],
+                y_tiles[t][:].indirect(enz_t[:, h * (HALF // 16) : (h + 1) * (HALF // 16)]),
+                rate[:, t, h * HALF : (h + 1) * HALF],
+                ALU.mult,
+            )
+
+        nc.vector.tensor_tensor(rate[:, 0:2, :], sb[:, 0:2, :], invs[0][:], ALU.mult)
+        cand_s = deal_bytes(cand_s_raw, "cand_s", "root0")
+        speeds_times_rates(0, 0)
+        speeds_times_rates(0, 1)
+        nc.vector.tensor_tensor(rate[:, 2:4, :], sb[:, 2:4, :], invs[1][:], ALU.mult)
+        cand_w = keep.tile([P, C], I32, name="cand_w", tag="root1", align_bytes=64)
         nc.vector.tensor_copy(
             cand_w[:].rearrange("p (t c i) -> p c t i", t=PACK, i=4),
             cand_w_raw[:].bitcast(I32).rearrange("p (c i t) -> p c t i", t=PACK, i=4),
         )
+        speeds_times_rates(0, 2)
+        speeds_times_rates(0, 3)
+        z32[1] = keep.tile([P, PACK, HALF], F32, name="z32_1", tag="inv1")
+        for t in range(PACK):
+            speeds_times_rates(1, t)
+
+        z16 = [keep.tile([P, HALF * PACK], BF16, name="z16_%d" % h, align_bytes=64) for h in range(2)]
+        nc.scalar.copy(
+            z16[0][:].rearrange("p (c i t) -> p c t i", i=2, t=PACK),
+            z32[0][:].rearrange("p t (c i) -> p c t i", i=2),
+        )
+        for u in range(2):
+            nc.scalar.copy(
+                z16[1][:].rearrange("p (v u e) -> p u v e", u=2, e=2)[:, u],
+                z32[1][:, 2 * u : 2 * u + 2, :].rearrange("p e v -> p v e"),
+            )
 
         z_codes = keep.tile([P, V], U32, name="z_codes", align_bytes=64)
         z_scales = keep.tile([P, V], U8, name="z_scales", align_bytes=64)
@@ -150,17 +184,7 @@ def tile_picked_enzyme_none_po_kernel(tc, x_words, x_scales, w1_words, w1_scales
         accs = []
         for h in range(2):
             cols = slice(h * HALF, (h + 1) * HALF)
-            num = keep.tile([P, PACK, HALF], F32, name="num%d" % h, tag=("num", "root")[h])
-            for t in range(PACK):
-                nc.vector.tensor_tensor(num[:, t, :], y_tiles[t][:].indirect(enz_t[:, h * (HALF // 16) : (h + 1) * (HALF // 16)]), sb[:, t, cols], ALU.mult)
-            z_h = keep.tile([P, HALF * PACK], BF16, name="z16_%d" % h, align_bytes=64)
-            nc.vector.tensor_tensor(
-                z_h[:].rearrange("p (c i t) -> p c t i", i=2, t=PACK),
-                num[:].rearrange("p t (c i) -> p c t i", i=2),
-                inv[:, :, cols].rearrange("p t (c i) -> p c t i", i=2),
-                ALU.mult,
-            )
-            nc.vector.quantize_mx(out=z_codes[:, cols].bitcast(FP8X4), scales=z_scales[:, cols], in_=z_h[:])
+            nc.vector.quantize_mx(out=z_codes[:, cols].bitcast(FP8X4), scales=z_scales[:, cols], in_=z16[h][:])
             banks = [psum.tile([P, S], F32, name="acc") for b in range(h + 1)]
             per_bank = PACK // len(banks)
             for t in range(PACK):
@@ -174,22 +198,36 @@ def tile_picked_enzyme_none_po_kernel(tc, x_words, x_scales, w1_words, w1_scales
                     stop=True,
                 )
             accs.append(banks)
-        for h in range(2):
+
+        o16 = [keep.tile([P, HALF * PACK], BF16, name="o16_%d" % h, align_bytes=64) for h in range(2)]
+
+        def store_planes(h):
             cols = slice(h * HALF, (h + 1) * HALF)
-            banks = accs[h]
-            per_bank = PACK // len(banks)
-            o32 = keep.tile([P, PACK * HALF], F32, name="o32_%d" % h)
-            for b, bank in enumerate(banks):
-                nc.scalar.activation(o32[:, b * per_bank * HALF : (b + 1) * per_bank * HALF], bank[:, : per_bank * HALF], ACT.Copy, scale=0.0625)
-            nc.scalar.dma_start(out_rows[:, :, cols], o32[:].rearrange("p (t v) -> p t v", t=PACK))
-            o16 = keep.tile([P, HALF * PACK], BF16, name="o16_%d" % h, align_bytes=64)
-            o16_v = o16[:].rearrange("p (c i t) -> p c t i", i=2, t=PACK)
-            o32_v = o32[:].rearrange("p (t c i) -> p c t i", i=2, t=PACK)
-            if h == 0:
-                nc.scalar.copy(o16_v, o32_v)
-            else:
-                nc.vector.tensor_copy(o16_v, o32_v)
-            nc.vector.quantize_mx(out=o_codes[:, cols].bitcast(FP8X4), scales=o_scales[:, cols], in_=o16[:])
-            nc.sync.dma_start(words_out[:, cols], o_codes[:, cols].bitcast(I32))
+            nc.vector.quantize_mx(out=o_codes[:, cols].bitcast(FP8X4), scales=o_scales[:, cols], in_=o16[h][:])
+
+        o32_0 = keep.tile([P, PACK * HALF], F32, name="o32_0")
+        nc.scalar.activation(o32_0[:], accs[0][0][:], ACT.Copy, scale=0.0625)
+        nc.sync.dma_start(out_rows[:, :, 0:HALF], o32_0[:].rearrange("p (t v) -> p t v", t=PACK))
+        nc.vector.tensor_copy(
+            o16[0][:].rearrange("p (c i t) -> p c t i", i=2, t=PACK),
+            o32_0[:].rearrange("p (t c i) -> p c t i", i=2, t=PACK),
+        )
+
+        for u in range(2):
+            nc.scalar.activation(
+                o16[1][:].rearrange("p (v u e) -> p u v e", u=2, e=2)[:, u],
+                accs[1][u][:, : 2 * HALF].rearrange("p (e v) -> p v e", e=2),
+                ACT.Copy,
+                scale=0.0625,
+            )
+        o32_a = keep.tile([P, 2 * HALF], F32, name="o32_a")
+        nc.vector.tensor_scalar_mul(o32_a[:], accs[1][0][:, : 2 * HALF], 0.0625)
+        nc.sync.dma_start(out_rows[:, 0:2, HALF:V], o32_a[:].rearrange("p (t v) -> p t v", t=2))
+        store_planes(0)
+        store_planes(1)
+        nc.sync.dma_start(words_out, o_codes[:].bitcast(I32))
+        o32_b = keep.tile([P, 2 * HALF], F32, name="o32_b")
+        nc.scalar.activation(o32_b[:], accs[1][1][:, : 2 * HALF], ACT.Copy, scale=0.0625)
+        nc.scalar.dma_start(out_rows[:, 2:4, HALF:V], o32_b[:].rearrange("p (t v) -> p t v", t=2))
         for q in range(4):
             (nc.sync, nc.scalar)[q % 2].dma_start(out_2[0, 4 * q : 4 * q + 4, :].bitcast(I32), o_scales[32 * q : 32 * q + 4, :].bitcast(I32))

@@ -55,9 +55,9 @@ def tile_picked_enzyme_none_po_kernel(tc, x_words, x_scales, w1_words, w1_scales
         load_scale_rows(xs, x_scales, nc.sync)
         offs_l = load_list(offs, "offs_l")
         cand_l = load_list(cand, "cand_l")
-        load_scale_rows(w2s_raw, w2_scales, nc.sync)
         xw = keep.tile([P, T], I32, name="xw", align_bytes=64)
         nc.sync.dma_start(xw[:], x_words[0].rearrange("p n t -> p (n t)").bitcast(I32))
+        load_scale_rows(w2s_raw, w2_scales, nc.sync)
         load_scale_rows(w1s_raw, w1_scales, nc.sync)
         sub_t = load_list(sub_l, "sub_t")
         inh_t = load_list(inh, "inh_t")
@@ -80,21 +80,21 @@ def tile_picked_enzyme_none_po_kernel(tc, x_words, x_scales, w1_words, w1_scales
             nc.vector.tensor_copy(t[:].rearrange("p (t m b) -> p t m b", t=PACK, b=2), raw[:].rearrange("p (m t b) -> p t m b", t=PACK, b=2))
             return t
 
-        def deal_bytes(raw, name, tag):
+        def deal_bytes(raw, name, tag, engine):
             t = keep.tile([P, S], U8, name=name, tag=tag, align_bytes=64)
-            nc.vector.tensor_copy(t[:].rearrange("p (t m) -> p t m", t=PACK), raw[:].rearrange("p (m t) -> p t m", t=PACK))
+            engine.tensor_copy(t[:].rearrange("p (t m) -> p t m", t=PACK), raw[:].rearrange("p (m t) -> p t m", t=PACK))
             return t
 
         w2w = deal_fp4(w2w_raw, "w2w")
         w1w = deal_fp4(w1w_raw, "w1w")
         two_s = gather_bytes(two_l, "two_s")
         offs_s = gather_bytes(offs_l, "offs_s")
-        w2s = deal_bytes(w2s_raw, "w2s", "w2s")
+        w2s = deal_bytes(w2s_raw, "w2s", "w2s", nc.gpsimd)
         cand_s_raw = gather_bytes(cand_l, "cand_s_raw")
         two_w = gather_words(two_l, "two_w", "two_w")
-        w1s = deal_bytes(w1s_raw, "w1s", "w1s")
-        offs_w = gather_words(offs_l, "offs_w", "w2s_raw")
-        cand_w_raw = gather_words(cand_l, "cand_w_raw", "w1s_raw")
+        w1s = deal_bytes(w1s_raw, "w1s", "w1s", nc.gpsimd)
+        offs_w = gather_words(offs_l, "offs_w", "offs_w")
+        cand_w_raw = gather_words(cand_l, "cand_w_raw", "cand_w_raw")
 
         def project(ww, ws, xg_w, xg_s, t):
             acc = psum.tile([P, S], F32, name="acc")
@@ -149,7 +149,7 @@ def tile_picked_enzyme_none_po_kernel(tc, x_words, x_scales, w1_words, w1_scales
             )
 
         nc.vector.tensor_tensor(rate[:, 0:2, :], sb[:, 0:2, :], invs[0][:], ALU.mult)
-        cand_s = deal_bytes(cand_s_raw, "cand_s", "root0")
+        cand_s = deal_bytes(cand_s_raw, "cand_s", "root0", nc.vector)
         speeds_times_rates(0, 0)
         speeds_times_rates(0, 1)
         nc.vector.tensor_tensor(rate[:, 2:4, :], sb[:, 2:4, :], invs[1][:], ALU.mult)

from contextlib import ExitStack

import concourse.mybir as mybir

K, T, S, V, H, C = 512, 2048, 512, 256, 512, 512
FLOPS = 2 * K * H * S * 2 + 2 * K * C * V

F32 = mybir.dt.float32
BF16 = mybir.dt.bfloat16
I32 = mybir.dt.int32
U32 = mybir.dt.uint32
U16 = mybir.dt.uint16
U8 = mybir.dt.uint8
FP8X4 = mybir.dt.float8_e4m3fn_x4
FP4X4 = mybir.dt.float4_e2m1fn_x4
ACT = mybir.ActivationFunctionType
ALU = mybir.AluOpType

P = 128
PACK = 4
HALF = V // 2


def tile_picked_enzyme_none_po_kernel(tc, x_words, x_scales, w1_words, w1_scales, w2_words, w2_scales, gs, offs, two, sub_l, enz, inh, cand, out_0, out_1, out_2):
    nc = tc.nc
    with ExitStack() as ctx:
        keep = ctx.enter_context(tc.tile_pool(name="keep", bufs=1))
        psum = ctx.enter_context(tc.psum_pool(name="psum", bufs=8))

        def load_scale_rows(plane, rows, queue):
            for q in range(4):
                queue.dma_start(plane[32 * q : 32 * q + 4, :].bitcast(I32), rows[0, 4 * q : 4 * q + 4, :].bitcast(I32))

        def load_list(src, name):
            t = keep.tile(list(src.shape), U16, name=name)
            nc.sync.dma_start(t[:], src)
            return t

        xs = keep.tile([P, T], U8, name="xs", align_bytes=64)
        nc.vector.memset(xs[:].bitcast(I32), 0)
        w2s_raw = keep.tile([P, H], U8, name="w2s_raw", align_bytes=64)
        w1s_raw = keep.tile([P, H], U8, name="w1s_raw", align_bytes=64)
        nc.vector.memset(w2s_raw[:].bitcast(I32), 0)
        nc.vector.memset(w1s_raw[:].bitcast(I32), 0)
        one = keep.tile([P, 1], F32, name="one")
        nc.vector.memset(one[:], 1.0)
        warm = keep.tile([P, 1], F32, name="warm")
        nc.scalar.activation(warm[:], one[:], ACT.Abs_reciprocal_sqrt, bias=0.5)

        w2w_raw = keep.tile([P, 2 * H], U8, name="w2w_raw", align_bytes=64)
        nc.sync.dma_start(w2w_raw[:].bitcast(I32), w2_words[0].bitcast(I32))
        w1w_raw = keep.tile([P, 2 * H], U8, name="w1w_raw", align_bytes=64)
        nc.sync.dma_start(w1w_raw[:].bitcast(I32), w1_words[0].bitcast(I32))
        two_l = load_list(two, "two_l")
        load_scale_rows(xs, x_scales, nc.sync)
        offs_l = load_list(offs, "offs_l")
        cand_l = load_list(cand, "cand_l")
        xw = keep.tile([P, T], I32, name="xw", align_bytes=64)
        nc.sync.dma_start(xw[:], x_words[0].rearrange("p n t -> p (n t)").bitcast(I32))
        load_scale_rows(w2s_raw, w2_scales, nc.sync)
        load_scale_rows(w1s_raw, w1_scales, nc.sync)
        sub_t = load_list(sub_l, "sub_t")
        inh_t = load_list(inh, "inh_t")
        gs_t = keep.tile([P, PACK], F32, name="gs_t")
        nc.sync.dma_start(gs_t[:], gs.rearrange("(p t) o -> p (t o)", t=PACK))
        enz_t = load_list(enz, "enz_t")

        def gather_bytes(lst, name):
            t = keep.tile([P, S], U8, name=name, align_bytes=64)
            nc.vector.tensor_copy(t[:], xs[:].indirect(lst[:]))
            return t

        def gather_words(lst, name, tag):
            t = keep.tile([P, S], U32, name=name, tag=tag, align_bytes=64)
            nc.vector.tensor_copy(t[:], xw[:].bitcast(U32).indirect(lst[:]))
            return t

        def deal_fp4(raw, name):
            t = keep.tile([P, 2 * H], U8, name=name, align_bytes=64)
            nc.vector.tensor_copy(t[:].rearrange("p (t m b) -> p t m b", t=PACK, b=2), raw[:].rearrange("p (m t b) -> p t m b", t=PACK, b=2))
            return t

        def deal_bytes(raw, name, tag, engine):
            t = keep.tile([P, S], U8, name=name, tag=tag, align_bytes=64)
            engine.tensor_copy(t[:].rearrange("p (t m) -> p t m", t=PACK), raw[:].rearrange("p (m t) -> p t m", t=PACK))
            return t

        w2w = deal_fp4(w2w_raw, "w2w")
        w1w = deal_fp4(w1w_raw, "w1w")
        two_s = gather_bytes(two_l, "two_s")
        offs_s = gather_bytes(offs_l, "offs_s")
        w2s = deal_bytes(w2s_raw, "w2s", "w2s", nc.gpsimd)
        cand_s_raw = gather_bytes(cand_l, "cand_s_raw")
        two_w = gather_words(two_l, "two_w", "two_w")
        w1s = deal_bytes(w1s_raw, "w1s", "w1s", nc.gpsimd)
        offs_w = gather_words(offs_l, "offs_w", "offs_w")
        cand_w_raw = gather_words(cand_l, "cand_w_raw", "cand_w_raw")

        def project(ww, ws, xg_w, xg_s, t):
            acc = psum.tile([P, S], F32, name="acc")
            nc.tensor.matmul_mx(
                out=acc[:],
                lhsT=ww[:, 2 * P * t : 2 * P * (t + 1)].bitcast(FP4X4),
                lhsT_scale=ws[:, P * t : P * (t + 1)],
                rhs=xg_w[:].bitcast(FP8X4),
                rhs_scale=xg_s[:],
                start=True,
                stop=True,
            )
            return acc

        c_tiles, y_tiles = [], []
        for t in range(PACK):
            acc = project(w2w, w2s, two_w, two_s, t)
            c_t = keep.tile([P, S], F32, name="c%d" % t)
            nc.scalar.activation(c_t[:], acc[:], ACT.Square)
            c_tiles.append(c_t)
        y_accs = [project(w1w, w1s, offs_w, offs_s, t) for t in range(PACK)]

        def scale_y(t):
            y_t = keep.tile([P, S], F32, name="y%d" % t)
            nc.scalar.activation(y_t[:], y_accs[t][:], ACT.Copy, scale=gs_t[:, t : t + 1])
            y_tiles.append(y_t)

        for t in range(PACK - 1):
            scale_y(t)

        sb = keep.tile([P, PACK, V], F32, name="sb")
        tot = keep.tile([P, PACK, V], F32, name="tot", tag="w1w", align_bytes=64)
        roots = [keep.tile([P, 2, V], F32, name="root%d" % u, align_bytes=64) for u in range(2)]
        invs = [keep.tile([P, 2, V], F32, name="inv%d" % u) for u in range(2)]
        for t in range(PACK):
            nc.vector.tensor_copy(sb[:, t, :], c_tiles[t][:].indirect(sub_t[:]))
        for t in range(PACK):
            nc.vector.tensor_tensor(tot[:, t, :], c_tiles[t][:].indirect(inh_t[:]), sb[:, t, :], ALU.add)
            nc.scalar.activation(roots[t // 2][:, t % 2, :], tot[:, t, :], ACT.Abs_reciprocal_sqrt, bias=0.5)
            nc.scalar.activation(invs[t // 2][:, t % 2, :], roots[t // 2][:, t % 2, :], ACT.Square)
        scale_y(PACK - 1)

        rate = keep.tile([P, PACK, V], F32, name="rate")
        z32 = [keep.tile([P, PACK, HALF], F32, name="z32_0"), None]

        def speeds_times_rates(h, t):
            nc.vector.tensor_tensor(
                z32[h][:, t, :],
                y_tiles[t][:].indirect(enz_t[:, h * (HALF // 16) : (h + 1) * (HALF // 16)]),
                rate[:, t, h * HALF : (h + 1) * HALF],
                ALU.mult,
            )

        nc.vector.tensor_tensor(rate[:, 0:2, :], sb[:, 0:2, :], invs[0][:], ALU.mult)
        cand_s = deal_bytes(cand_s_raw, "cand_s", "root0", nc.vector)
        speeds_times_rates(0, 0)
        speeds_times_rates(0, 1)
        nc.vector.tensor_tensor(rate[:, 2:4, :], sb[:, 2:4, :], invs[1][:], ALU.mult)
        cand_w = keep.tile([P, C], I32, name="cand_w", tag="root1", align_bytes=64)
        nc.vector.tensor_copy(
            cand_w[:].rearrange("p (t c i) -> p c t i", t=PACK, i=4),
            cand_w_raw[:].bitcast(I32).rearrange("p (c i t) -> p c t i", t=PACK, i=4),
        )
        speeds_times_rates(0, 2)
        speeds_times_rates(0, 3)
        z32[1] = keep.tile([P, PACK, HALF], F32, name="z32_1", tag="inv1")
        for t in range(PACK):
            speeds_times_rates(1, t)

        z16 = [keep.tile([P, HALF * PACK], BF16, name="z16_%d" % h, align_bytes=64) for h in range(2)]
        nc.scalar.copy(
            z16[0][:].rearrange("p (c i t) -> p c t i", i=2, t=PACK),
            z32[0][:].rearrange("p t (c i) -> p c t i", i=2),
        )
        for u in range(2):
            nc.scalar.copy(
                z16[1][:].rearrange("p (v u e) -> p u v e", u=2, e=2)[:, u],
                z32[1][:, 2 * u : 2 * u + 2, :].rearrange("p e v -> p v e"),
            )

        z_codes = keep.tile([P, V], U32, name="z_codes", align_bytes=64)
        z_scales = keep.tile([P, V], U8, name="z_scales", align_bytes=64)
        o_codes = keep.tile([P, V], U32, name="o_codes", align_bytes=64)
        o_scales = keep.tile([P, V], U8, name="o_scales", align_bytes=64)
        out_rows = out_0.rearrange("(p t) v -> p t v", t=PACK)
        words_out = out_1[0].rearrange("p n t -> p (n t)").bitcast(I32)
        accs = []
        for h in range(2):
            cols = slice(h * HALF, (h + 1) * HALF)
            nc.vector.quantize_mx(out=z_codes[:, cols].bitcast(FP8X4), scales=z_scales[:, cols], in_=z16[h][:])
            banks = [psum.tile([P, S], F32, name="acc") for b in range(h + 1)]
            per_bank = PACK // len(banks)
            for t in range(PACK):
                nc.tensor.matmul_mx(
                    out=banks[t // per_bank][:, (t % per_bank) * HALF : (t % per_bank + 1) * HALF],
                    lhsT=cand_w[:, P * t : P * (t + 1)].bitcast(FP8X4),
                    lhsT_scale=cand_s[:, P * t : P * (t + 1)],
                    rhs=z_codes[:, cols].bitcast(FP8X4),
                    rhs_scale=z_scales[:, cols],
                    start=True,
                    stop=True,
                )
            accs.append(banks)

        o16 = [keep.tile([P, HALF * PACK], BF16, name="o16_%d" % h, align_bytes=64) for h in range(2)]

        def store_planes(h):
            cols = slice(h * HALF, (h + 1) * HALF)
            nc.vector.quantize_mx(out=o_codes[:, cols].bitcast(FP8X4), scales=o_scales[:, cols], in_=o16[h][:])

        o32_0 = keep.tile([P, PACK * HALF], F32, name="o32_0")
        nc.scalar.activation(o32_0[:], accs[0][0][:], ACT.Copy, scale=0.0625)
        nc.sync.dma_start(out_rows[:, :, 0:HALF], o32_0[:].rearrange("p (t v) -> p t v", t=PACK))
        nc.vector.tensor_copy(
            o16[0][:].rearrange("p (c i t) -> p c t i", i=2, t=PACK),
            o32_0[:].rearrange("p (t c i) -> p c t i", i=2, t=PACK),
        )

        for u in range(2):
            nc.scalar.activation(
                o16[1][:].rearrange("p (v u e) -> p u v e", u=2, e=2)[:, u],
                accs[1][u][:, : 2 * HALF].rearrange("p (e v) -> p v e", e=2),
                ACT.Copy,
                scale=0.0625,
            )
        o32_a = keep.tile([P, 2 * HALF], F32, name="o32_a")
        nc.vector.tensor_scalar_mul(o32_a[:], accs[1][0][:, : 2 * HALF], 0.0625)
        nc.sync.dma_start(out_rows[:, 0:2, HALF:V], o32_a[:].rearrange("p (t v) -> p t v", t=2))
        store_planes(0)
        store_planes(1)
        nc.sync.dma_start(words_out, o_codes[:].bitcast(I32))
        o32_b = keep.tile([P, 2 * HALF], F32, name="o32_b")
        nc.scalar.activation(o32_b[:], accs[1][1][:, : 2 * HALF], ACT.Copy, scale=0.0625)
        nc.scalar.dma_start(out_rows[:, 2:4, HALF:V], o32_b[:].rearrange("p (t v) -> p t v", t=2))
        for q in range(4):
            (nc.sync, nc.scalar)[q % 2].dma_start(out_2[0, 4 * q : 4 * q + 4, :].bitcast(I32), o_scales[32 * q : 32 * q + 4, :].bitcast(I32))
